import numpy as np
import ml_dtypes


def mxq(x, axis, fmt="e4m3"):
    dtype, down = {"e4m3": (ml_dtypes.float8_e4m3fn, 7), "e5m2": (ml_dtypes.float8_e5m2, 14)}[fmt]
    v = np.moveaxis(np.asarray(x, np.float32).astype(ml_dtypes.bfloat16).astype(np.float64), axis, -1)
    blocks = v.reshape(v.shape[:-1] + (-1, 32))
    amax = np.abs(blocks).max(-1, keepdims=True)
    byte = np.maximum(np.where(amax > 0, np.frexp(amax)[1] - 1 + 127, 0) - down, 1)
    scale = np.exp2(byte - 127.0)
    codes = (blocks / scale).astype(np.float32).astype(dtype).astype(np.float64)
    return np.moveaxis((codes * scale).reshape(v.shape), -1, axis)


WIDE = False


def mx_kscale(k):
    if not WIDE:
        return np.ones(k)
    levels = np.array([10, -10, 5, -5, 0])
    if k % 512:
        return np.exp2(np.random.permutation(np.resize(levels, k // 32))).repeat(32)
    a = np.empty((k // 512, 16))
    for p in range(k // 512):
        a[p, :8] = np.random.permutation(np.resize(levels, 8))
        for g in range(8):
            far = levels[np.abs(levels - a[p, g]) >= 10]
            a[p, g + 8] = far[np.random.randint(len(far))]
    return np.exp2(a.ravel()).repeat(32)


def f64(x):
    return np.asarray(x).astype(np.float64)


def striped(idx):
    return np.tile(idx.reshape(-1, 16).T, (8, 1)).astype(np.uint16)


def unstriped(offs):
    return offs[:16].T.reshape(-1).astype(np.int64)


def striped8(idx):
    return np.concatenate([x.reshape(-1, 16).T for x in idx]).astype(np.uint16)


def runs(offs, k):
    lists = np.stack([offs[16 * r : 16 * r + 16].T.reshape(-1) for r in range(8)]).astype(np.int64)
    return lists[np.arange(k) % 512 // 64]


def pack_weight(w):
    k, n = w.shape
    w = f64(np.asarray(w, np.float32).astype(ml_dtypes.bfloat16)).reshape(k // 32, 32, n)
    amax = np.abs(w).max(1)
    byte = np.clip(np.where(amax > 0, np.frexp(amax)[1] - 1 + 127 - 7, 1), 1, 254)
    scaled = (w * np.exp2(127.0 - byte)[:, None, :]).reshape(k, n).astype(np.float32)
    words = np.ascontiguousarray(scaled.reshape(k // 512, 128, 4, n).transpose(0, 1, 3, 2)).astype(ml_dtypes.float8_e4m3fn).view(np.uint8)
    return words, np.ascontiguousarray(byte.astype(np.uint8).reshape(k // 512, 16, n))


def unpack_weight(words, scales):
    g, p, n, _ = words.shape
    vals = np.ascontiguousarray(words).view(ml_dtypes.float8_e4m3fn).astype(np.float64) * np.repeat(np.exp2(scales.astype(np.float64) - 127.0), 8, axis=1)[..., None]
    return vals.transpose(0, 1, 3, 2).reshape(g * 512, n)


def relu(v):
    return np.maximum(v, 0.0)


def sigmoid(v):
    return 1.0 / (1.0 + np.exp(-np.maximum(v, -700.0)))

def planes(y):
    n, m = y.shape
    v = y.astype(np.float32).astype(ml_dtypes.bfloat16).astype(np.float64).reshape(n // 32, 32, m)
    top = np.abs(v).max(1)
    byte = np.clip(np.where(top > 0, np.frexp(top)[1] - 1 + 127 - 7, 1), 1, 254)
    codes = (v * np.exp2(127.0 - byte)[:, None, :]).reshape(n, m).astype(np.float32).astype(ml_dtypes.float8_e4m3fn).view(np.uint8)
    words = codes.reshape(n // 512, 128, 4, m).transpose(0, 1, 3, 2)
    return np.ascontiguousarray(words), np.ascontiguousarray(byte.astype(np.uint8).reshape(n // 512, 16, m))


K, T, S, V, H, C = 512, 2048, 512, 256, 512, 512


def setup_inputs():
    n = np.random.standard_normal
    s = mx_kscale(K)[:, None]
    packed_xT = pack_weight(n((K, T)) * s)
    packed_w1 = pack_weight(n((K, H)) / np.sqrt(K) / s)
    perm = np.stack([np.random.permutation(S) for _ in range(8)])
    return {
        "x_words": packed_xT[0],
        "x_scales": packed_xT[1],
        "w1_words": packed_w1[0],
        "w1_scales": packed_w1[1],
        "gs": (np.random.uniform(0.5, 1.5, (K, 1)) / s).astype(np.float32),
        "offs": striped(np.random.permutation(T)[:S]),
        "cand": striped(np.random.permutation(T)[:C]),
        "la": striped8(perm[:, :V]),
        "lb": striped8(perm[:, V:]),
    }


def reference(x_words, x_scales, w1_words, w1_scales, gs, offs, cand, la, lb):
    x_cand = unpack_weight(x_words, x_scales)[:, unstriped(cand)]
    xq = unpack_weight(x_words, x_scales)[:, unstriped(offs)]
    h = relu(unpack_weight(w1_words, w1_scales).T @ xq)
    z = f64(gs) * h
    s = 0.0625 * ((x_cand.T @ mxq(z, 0, "e4m3")))
    b = s[np.arange(C)[:, None], runs(lb, C)]
    a = s[np.arange(C)[:, None], runs(la, C)]
    t1 = sigmoid(a - b)
    nb = b * (-1.0 * t1 + 1)
    na = a * t1
    sp = np.zeros((C, S))
    sp[np.arange(C)[:, None], runs(la, C)] = na
    out = sp.copy()
    out[np.arange(C)[:, None], runs(lb, C)] = nb
    return (out,) + planes(out)

@@ -1,0 +1,223 @@
+from contextlib import ExitStack
+
+import concourse.mybir as mybir
+
+K, T, S, V, H, C = 512, 2048, 512, 256, 512, 512
+FLOPS = 2 * K * H * S + 2 * K * C * S
+
+F32 = mybir.dt.float32
+BF16 = mybir.dt.bfloat16
+I32 = mybir.dt.int32
+U32 = mybir.dt.uint32
+U16 = mybir.dt.uint16
+U8 = mybir.dt.uint8
+FP8X4 = mybir.dt.float8_e4m3fn_x4
+ALU = mybir.AluOpType
+ACT = mybir.ActivationFunctionType
+
+P = 128
+PACK = 4
+QUADS = 4
+NQ = 128
+ORDER = (0, 2, 3, 1)
+
+
+def tile_picked_candduel_none_po_kernel(
+    tc, x_words, x_scales, w1_words, w1_scales, gs, offs, cand, la, lb, out_0, out_1, out_2
+):
+    nc = tc.nc
+    with ExitStack() as ctx:
+        keep = ctx.enter_context(tc.tile_pool(name="keep", bufs=1))
+        psum = ctx.enter_context(tc.psum_pool(name="psum", bufs=1))
+
+        def sb(name, shape, dtype, tag=None):
+            return keep.tile(shape, dtype, name=name, tag=tag or name, align_bytes=64)
+
+        offs_t = sb("offs_t", [P, S // 16], U16)
+        cand_t = sb("cand_t", [P, C // 16], U16)
+        la_t = sb("la_t", [P, V // 16], U16)
+        lb_t = sb("lb_t", [P, V // 16], U16)
+        xw = sb("xw", [P, T], I32)
+        xs = sb("xs", [P, T], U8)
+        ww = sb("ww", [P, H], I32)
+        ws = sb("ws", [P, H], U8)
+        gs_t = sb("gs_t", [P, PACK], F32)
+        warm = sb("warm", [P, 2], F32)
+
+        nc.vector.memset(xs[:].bitcast(I32), 0)
+        nc.vector.memset(ws[:].bitcast(I32), 0)
+        nc.gpsimd.memset(warm[:, 0:1], 0.0)
+        nc.scalar.activation(warm[:, 1:2], warm[:, 0:1], ACT.Sigmoid)
+
+        nc.sync.dma_start(offs_t[:], offs)
+        nc.sync.dma_start(cand_t[:], cand)
+        nc.sync.dma_start(ww[:], w1_words[0].rearrange("p n t -> p (n t)").bitcast(I32))
+        for q in range(QUADS):
+            nc.sync.dma_start(xs[32 * q : 32 * q + 4, :].bitcast(I32), x_scales[0, 4 * q : 4 * q + 4, :].bitcast(I32))
+        nc.sync.dma_start(xw[:], x_words[0].rearrange("p n t -> p (n t)").bitcast(I32))
+        for q in range(QUADS):
+            nc.scalar.dma_start(ws[32 * q : 32 * q + 4, :].bitcast(I32), w1_scales[0, 4 * q : 4 * q + 4, :].bitcast(I32))
+        nc.sync.dma_start(gs_t[:], gs.rearrange("(p t) o -> p (t o)", t=PACK))
+        nc.sync.dma_start(la_t[:], la)
+        nc.sync.dma_start(lb_t[:], lb)
+
+        def deal(dst, src):
+            nc.vector.tensor_copy(
+                dst.rearrange("p (t m) -> p m t", t=PACK), src.rearrange("p (m t) -> p m t", t=PACK)
+            )
+
+        wwd = sb("wwd", [P, H], I32)
+        wsd = sb("wsd", [P, H], U8)
+        qs = sb("qs", [P, S], U8)
+        cs = sb("cs", [P, C], U8)
+        cs_first = sb("cs_first", [P, P], U8)
+        cw_first = sb("cw_first", [P, P], U32)
+        qw = [sb(f"qw{h}", [P, S // 2], U32) for h in range(2)]
+
+        deal(wwd[:], ww[:])
+        nc.vector.tensor_copy(qs[:], xs[:].indirect(offs_t[:]))
+        nc.vector.tensor_copy(cs[:], xs[:].indirect(cand_t[:]))
+        nc.vector.tensor_copy(cs_first[:], cs[:, 0:C:PACK])
+        nc.vector.tensor_copy(qw[0][:], xw[:].bitcast(U32).indirect(offs_t[:, 0:16]))
+        nc.vector.tensor_copy(qw[1][:], xw[:].bitcast(U32).indirect(offs_t[:, 16:32]))
+        deal(wsd[:], ws[:])
+        cw = sb("cw", [P, C], U32, tag="ws")
+        nc.vector.tensor_copy(cw[:], xw[:].bitcast(U32).indirect(cand_t[:]))
+        nc.vector.tensor_copy(cw_first[:], cw[:, 0:C:PACK])
+
+        nq = S // NQ
+        hb = []
+        for q in range(nq):
+            bank = psum.tile([P, PACK, NQ], F32, name=f"hb{q}", tag=f"bank{q}")
+            for t in range(PACK):
+                nc.tensor.matmul_mx(
+                    out=bank[:, t, :],
+                    lhsT=wwd[:, P * t : P * (t + 1)].bitcast(FP8X4),
+                    lhsT_scale=wsd[:, P * t : P * (t + 1)],
+                    rhs=qw[q // 2][:, NQ * (q % 2) : NQ * (q % 2 + 1)].bitcast(FP8X4),
+                    rhs_scale=qs[:, NQ * q : NQ * (q + 1)],
+                    start=True,
+                    stop=True,
+                )
+            hb.append(bank)
+
+        zb = [sb(f"zb{q}", [P, NQ, PACK], BF16) for q in range(nq)]
+        zw = [sb(f"zw{q}", [P, NQ], U32) for q in range(nq)]
+        zs = [sb(f"zs{q}", [P, NQ], U8) for q in range(nq)]
+
+        def make_z(q):
+            nc.vector.scalar_tensor_tensor(
+                zb[q][:],
+                hb[q][:].rearrange("p t n -> p n t"),
+                0.0,
+                gs_t[:].unsqueeze(1).to_broadcast([P, NQ, PACK]),
+                ALU.max,
+                ALU.mult,
+            )
+
+        def quant_z(q):
+            nc.vector.quantize_mx(
+                out=zw[q][:].bitcast(FP8X4), scales=zs[q][:], in_=zb[q][:].rearrange("p n t -> p (n t)")
+            )
+
+        make_z(0)
+        for q in range(1, nq):
+            make_z(q)
+            quant_z(q - 1)
+        quant_z(nq - 1)
+
+        def score(out, words, scales, q):
+            nc.tensor.matmul_mx(
+                out=out,
+                lhsT=words.bitcast(FP8X4),
+                lhsT_scale=scales,
+                rhs=zw[q][:].bitcast(FP8X4),
+                rhs_scale=zs[q][:],
+                start=True,
+                stop=True,
+            )
+
+        early = (nq - 1) * NQ
+        s_early = psum.tile([P, early], F32, name="s_early")
+        for q in range(nq - 1):
+            score(s_early[:, NQ * q : NQ * (q + 1)], cw_first[:], cs_first[:], q)
+        s_late = psum.tile([P, NQ], F32, name="s_late", tag="bank0")
+        score(s_late[:], cw_first[:], cs_first[:], nq - 1)
+
+        rest = PACK - 1
+        cs_rest = sb("cs_rest", [P, rest * P], U8, tag=f"zb{nq - 2}")
+        cw_rest = sb("cw_rest", [P, rest * P], U32, tag=f"zb{nq - 1}")
+        for dst, src in ((cs_rest, cs), (cw_rest, cw)):
+            nc.vector.tensor_copy(
+                dst[:].rearrange("p (t m) -> p m t", t=rest), src[:].rearrange("p (m t) -> p m t", t=PACK)[:, :, 1:PACK]
+            )
+        s_bank = {}
+        for t in ORDER[1:]:
+            s_bank[t] = psum.tile([P, S], F32, name=f"s_bank{t}")
+            cols = slice(P * (t - 1), P * t)
+            for q in range(nq):
+                score(s_bank[t][:, NQ * q : NQ * (q + 1)], cw_rest[:, cols], cs_rest[:, cols], q)
+
+        sw = {t: sb(f"sw{t}", [P, S], F32) for t in ORDER}
+        av = {t: sb(f"av{t}", [P, V], F32) for t in ORDER}
+        bv = {t: sb(f"bv{t}", [P, V], F32) for t in ORDER}
+        dv = {t: sb(f"dv{t}", [P, V], F32) for t in ORDER}
+        ta = {t: sb(f"ta{t}", [P, V], F32) for t in ORDER}
+        tb = {t: sb(f"tb{t}", [P, V], F32) for t in ORDER}
+        yw = {t: sb(f"yw{t}", [P, S], F32) for t in ORDER}
+
+        def diff(t):
+            nc.vector.tensor_tensor(dv[t][:], av[t][:], bv[t][:], ALU.subtract)
+            nc.scalar.activation(ta[t][:], dv[t][:], ACT.Sigmoid)
+            nc.scalar.activation(tb[t][:], dv[t][:], ACT.Sigmoid, scale=-1.0)
+
+        for i, t in enumerate(ORDER):
+            if i == 0:
+                nc.scalar.activation(sw[t][:, 0:early], s_early[:], ACT.Copy, scale=0.0625)
+                nc.scalar.activation(sw[t][:, early:S], s_late[:], ACT.Copy, scale=0.0625)
+            else:
+                nc.scalar.activation(sw[t][:], s_bank[t][:], ACT.Copy, scale=0.0625)
+            nc.vector.tensor_copy(av[t][:], sw[t][:].indirect(la_t[:]))
+            if i > 0:
+                diff(ORDER[i - 1])
+            nc.vector.tensor_copy(bv[t][:], sw[t][:].indirect(lb_t[:]))
+
+        half = S // 2
+        yb = [sb(f"yb{h}", [P, half, PACK], BF16) for h in range(2)]
+        yc = [sb(f"yc{h}", [P, half], I32) for h in range(2)]
+        ys = sb("ys", [P, S], U8)
+        rows = out_0.rearrange("(p t) c -> p t c", t=PACK)
+
+        def put_a(t):
+            nc.vector.tensor_tensor(yw[t][:].indirect(la_t[:]), av[t][:], ta[t][:], ALU.mult)
+
+        def put_b(t):
+            nc.vector.tensor_tensor(yw[t][:].indirect(lb_t[:]), bv[t][:], tb[t][:], ALU.mult)
+            nc.sync.dma_start(rows[:, t, :], yw[t][:])
+            for h in range(2):
+                cols = yw[t][:, half * h : half * (h + 1)]
+                if t == ORDER[-1]:
+                    nc.vector.tensor_copy(yb[h][:, :, t], cols)
+                elif t == ORDER[0]:
+                    nc.scalar.activation(yb[h][:, :, 0:2], cols.unsqueeze(2).to_broadcast([P, half, 2]), ACT.Copy)
+                else:
+                    nc.scalar.activation(yb[h][:, :, t], cols, ACT.Copy)
+
+        put_a(ORDER[0])
+        diff(ORDER[-1])
+        for i in range(1, PACK):
+            put_a(ORDER[i])
+            put_b(ORDER[i - 1])
+        put_b(ORDER[-1])
+
+        words_out = out_1[0].rearrange("p m t -> p (m t)").bitcast(I32)
+        for h in range(2):
+            nc.vector.quantize_mx(
+                out=yc[h][:].bitcast(FP8X4),
+                scales=ys[:, half * h : half * (h + 1)],
+                in_=yb[h][:].rearrange("p n t -> p (n t)"),
+            )
+            nc.sync.dma_start(words_out[:, half * h : half * (h + 1)], yc[h][:])
+        for q in range(QUADS):
+            eng = nc.scalar if q % 2 else nc.sync
+            eng.dma_start(out_2[0, 4 * q : 4 * q + 4, :].bitcast(I32), ys[32 * q : 32 * q + 4, :].bitcast(I32))

@@ -46,7 +46,7 @@ def tile_picked_candduel_none_po_kernel(
 
         nc.vector.memset(xs[:].bitcast(I32), 0)
         nc.vector.memset(ws[:].bitcast(I32), 0)
-        nc.gpsimd.memset(warm[:, 0:1], 0.0)
+        nc.vector.memset(warm[:, 0:1], 0.0)
         nc.scalar.activation(warm[:, 1:2], warm[:, 0:1], ACT.Sigmoid)
 
         nc.sync.dma_start(offs_t[:], offs)
@@ -56,7 +56,7 @@ def tile_picked_candduel_none_po_kernel(
             nc.sync.dma_start(xs[32 * q : 32 * q + 4, :].bitcast(I32), x_scales[0, 4 * q : 4 * q + 4, :].bitcast(I32))
         nc.sync.dma_start(xw[:], x_words[0].rearrange("p n t -> p (n t)").bitcast(I32))
         for q in range(QUADS):
-            nc.scalar.dma_start(ws[32 * q : 32 * q + 4, :].bitcast(I32), w1_scales[0, 4 * q : 4 * q + 4, :].bitcast(I32))
+            nc.sync.dma_start(ws[32 * q : 32 * q + 4, :].bitcast(I32), w1_scales[0, 4 * q : 4 * q + 4, :].bitcast(I32))
         nc.sync.dma_start(gs_t[:], gs.rearrange("(p t) o -> p (t o)", t=PACK))
         nc.sync.dma_start(la_t[:], la)
         nc.sync.dma_start(lb_t[:], lb)
@@ -72,26 +72,27 @@ def tile_picked_candduel_none_po_kernel(
         cs = sb("cs", [P, C], U8)
         cs_first = sb("cs_first", [P, P], U8)
         cw_first = sb("cw_first", [P, P], U32)
-        qw = [sb(f"qw{h}", [P, S // 2], U32) for h in range(2)]
 
         deal(wwd[:], ww[:])
         nc.vector.tensor_copy(qs[:], xs[:].indirect(offs_t[:]))
         nc.vector.tensor_copy(cs[:], xs[:].indirect(cand_t[:]))
-        nc.vector.tensor_copy(cs_first[:], cs[:, 0:C:PACK])
-        nc.vector.tensor_copy(qw[0][:], xw[:].bitcast(U32).indirect(offs_t[:, 0:16]))
+        qw = {1: sb("qw1", [P, S // 2], U32)}
         nc.vector.tensor_copy(qw[1][:], xw[:].bitcast(U32).indirect(offs_t[:, 16:32]))
         deal(wsd[:], ws[:])
-        cw = sb("cw", [P, C], U32, tag="ws")
+        nc.vector.tensor_copy(cs_first[:], cs[:, 0:C:PACK])
+        later = sb("later", [P, S // 2 + C], U32, tag="ws")
+        qw[0] = later[:, 0 : S // 2]
+        cw = later[:, S // 2 :]
+        nc.vector.tensor_copy(qw[0][:], xw[:].bitcast(U32).indirect(offs_t[:, 0:16]))
         nc.vector.tensor_copy(cw[:], xw[:].bitcast(U32).indirect(cand_t[:]))
-        nc.vector.tensor_copy(cw_first[:], cw[:, 0:C:PACK])
 
         nq = S // NQ
-        hb = []
-        for q in range(nq):
-            bank = psum.tile([P, PACK, NQ], F32, name=f"hb{q}", tag=f"bank{q}")
+        hb = {}
+        for q in (2, 3, 0, 1):
+            hb[q] = psum.tile([P, PACK, NQ], F32, name=f"hb{q}", tag=f"bank{q}")
             for t in range(PACK):
                 nc.tensor.matmul_mx(
-                    out=bank[:, t, :],
+                    out=hb[q][:, t, :],
                     lhsT=wwd[:, P * t : P * (t + 1)].bitcast(FP8X4),
                     lhsT_scale=wsd[:, P * t : P * (t + 1)],
                     rhs=qw[q // 2][:, NQ * (q % 2) : NQ * (q % 2 + 1)].bitcast(FP8X4),
@@ -99,32 +100,32 @@ def tile_picked_candduel_none_po_kernel(
                     start=True,
                     stop=True,
                 )
-            hb.append(bank)
 
         zb = [sb(f"zb{q}", [P, NQ, PACK], BF16) for q in range(nq)]
         zw = [sb(f"zw{q}", [P, NQ], U32) for q in range(nq)]
         zs = [sb(f"zs{q}", [P, NQ], U8) for q in range(nq)]
+        gains = gs_t[:].unsqueeze(1).to_broadcast([P, NQ, PACK])
 
         def make_z(q):
-            nc.vector.scalar_tensor_tensor(
-                zb[q][:],
-                hb[q][:].rearrange("p t n -> p n t"),
-                0.0,
-                gs_t[:].unsqueeze(1).to_broadcast([P, NQ, PACK]),
-                ALU.max,
-                ALU.mult,
-            )
+            nc.vector.scalar_tensor_tensor(zb[q][:], hb[q][:].rearrange("p t n -> p n t"), 0.0, gains, ALU.max, ALU.mult)
+
+        def make_z_aside(q):
+            hr = sb(f"hr{q}", [P, NQ, PACK], F32)
+            nc.scalar.activation(hr[:], hb[q][:].rearrange("p t n -> p n t"), ACT.Relu)
+            nc.gpsimd.tensor_tensor(zb[q][:], hr[:], gains, ALU.mult)
 
         def quant_z(q):
             nc.vector.quantize_mx(
                 out=zw[q][:].bitcast(FP8X4), scales=zs[q][:], in_=zb[q][:].rearrange("p n t -> p (n t)")
             )
 
+        make_z_aside(2)
+        make_z_aside(3)
         make_z(0)
-        for q in range(1, nq):
-            make_z(q)
-            quant_z(q - 1)
-        quant_z(nq - 1)
+        nc.vector.tensor_copy(cw_first[:], cw[:, 0:C:PACK])
+        make_z(1)
+        for q in (0, 2, 1, 3):
+            quant_z(q)
 
         def score(out, words, scales, q):
             nc.tensor.matmul_mx(
@@ -139,13 +140,13 @@ def tile_picked_candduel_none_po_kernel(
 
         early = (nq - 1) * NQ
         s_early = psum.tile([P, early], F32, name="s_early")
-        for q in range(nq - 1):
+        for q in (0, 2, 1):
             score(s_early[:, NQ * q : NQ * (q + 1)], cw_first[:], cs_first[:], q)
-        s_late = psum.tile([P, NQ], F32, name="s_late", tag="bank0")
+        s_late = psum.tile([P, NQ], F32, name="s_late", tag="bank2")
         score(s_late[:], cw_first[:], cs_first[:], nq - 1)
 
         rest = PACK - 1
-        cs_rest = sb("cs_rest", [P, rest * P], U8, tag=f"zb{nq - 2}")
+        cs_rest = sb("cs_rest", [P, rest * P], U8, tag="zb1")
         cw_rest = sb("cw_rest", [P, rest * P], U32, tag=f"zb{nq - 1}")
         for dst, src in ((cs_rest, cs), (cw_rest, cw)):
             nc.vector.tensor_copy(
@@ -167,7 +168,8 @@ def tile_picked_candduel_none_po_kernel(
         yw = {t: sb(f"yw{t}", [P, S], F32) for t in ORDER}
 
         def diff(t):
-            nc.vector.tensor_tensor(dv[t][:], av[t][:], bv[t][:], ALU.subtract)
+            eng = nc.vector if t == ORDER[-1] else nc.gpsimd
+            eng.tensor_tensor(dv[t][:], av[t][:], bv[t][:], ALU.subtract)
             nc.scalar.activation(ta[t][:], dv[t][:], ACT.Sigmoid)
             nc.scalar.activation(tb[t][:], dv[t][:], ACT.Sigmoid, scale=-1.0)
 
@@ -196,9 +198,9 @@ def tile_picked_candduel_none_po_kernel(
             nc.sync.dma_start(rows[:, t, :], yw[t][:])
             for h in range(2):
                 cols = yw[t][:, half * h : half * (h + 1)]
-                if t == ORDER[-1]:
+                if t == ORDER[-1] and h == 0:
                     nc.vector.tensor_copy(yb[h][:, :, t], cols)
-                elif t == ORDER[0]:
+                elif t == ORDER[0] and h == 0:
                     nc.scalar.activation(yb[h][:, :, 0:2], cols.unsqueeze(2).to_broadcast([P, half, 2]), ACT.Copy)
                 else:
                     nc.scalar.activation(yb[h][:, :, t], cols, ACT.Copy)

@@ -1,6 +1,7 @@
 from contextlib import ExitStack
 
 import concourse.mybir as mybir
+from concourse.masks import make_identity
 
 K, T, S, V, H, C = 512, 2048, 512, 256, 512, 512
 FLOPS = 2 * K * H * S + 2 * K * C * S
@@ -49,6 +50,9 @@ def tile_picked_candduel_none_po_kernel(
         nc.vector.memset(warm[:, 0:1], 0.0)
         nc.scalar.activation(warm[:, 1:2], warm[:, 0:1], ACT.Sigmoid)
 
+        ident = sb("ident", [P, P], F32, tag="warm")
+        make_identity(nc, ident[:])
+
         nc.sync.dma_start(offs_t[:], offs)
         nc.sync.dma_start(cand_t[:], cand)
         nc.sync.dma_start(ww[:], w1_words[0].rearrange("p n t -> p (n t)").bitcast(I32))
@@ -61,9 +65,9 @@ def tile_picked_candduel_none_po_kernel(
         nc.sync.dma_start(la_t[:], la)
         nc.sync.dma_start(lb_t[:], lb)
 
-        def deal(dst, src):
+        def deal(dst, src, first):
             nc.vector.tensor_copy(
-                dst.rearrange("p (t m) -> p m t", t=PACK), src.rearrange("p (m t) -> p m t", t=PACK)
+                dst.rearrange("p (t m) -> p m t", m=P), src.rearrange("p (m t) -> p m t", t=PACK)[:, :, first:PACK]
             )
 
         wwd = sb("wwd", [P, H], I32)
@@ -73,22 +77,23 @@ def tile_picked_candduel_none_po_kernel(
         cs_first = sb("cs_first", [P, P], U8)
         cw_first = sb("cw_first", [P, P], U32)
 
-        deal(wwd[:], ww[:])
+        deal(wwd[:], ww[:], 0)
         nc.vector.tensor_copy(qs[:], xs[:].indirect(offs_t[:]))
         nc.vector.tensor_copy(cs[:], xs[:].indirect(cand_t[:]))
-        qw = {1: sb("qw1", [P, S // 2], U32)}
-        nc.vector.tensor_copy(qw[1][:], xw[:].bitcast(U32).indirect(offs_t[:, 16:32]))
-        deal(wsd[:], ws[:])
-        nc.vector.tensor_copy(cs_first[:], cs[:, 0:C:PACK])
-        later = sb("later", [P, S // 2 + C], U32, tag="ws")
-        qw[0] = later[:, 0 : S // 2]
-        cw = later[:, S // 2 :]
+        qw = {0: sb("qw0", [P, S // 2], U32)}
         nc.vector.tensor_copy(qw[0][:], xw[:].bitcast(U32).indirect(offs_t[:, 0:16]))
+        deal(wsd[:], ws[:], 0)
+        later = sb("later", [P, S // 2 + C], U32, tag="ws")
+        qw[1] = later[:, 0 : S // 2]
+        cw = later[:, S // 2 :]
+        nc.vector.tensor_copy(qw[1][:], xw[:].bitcast(U32).indirect(offs_t[:, 16:32]))
         nc.vector.tensor_copy(cw[:], xw[:].bitcast(U32).indirect(cand_t[:]))
+        nc.vector.tensor_copy(cs_first[:], cs[:, 0:C:PACK])
+        nc.vector.tensor_copy(cw_first[:], cw[:, 0:C:PACK])
 
         nq = S // NQ
         hb = {}
-        for q in (2, 3, 0, 1):
+        for q in range(nq):
             hb[q] = psum.tile([P, PACK, NQ], F32, name=f"hb{q}", tag=f"bank{q}")
             for t in range(PACK):
                 nc.tensor.matmul_mx(
@@ -109,22 +114,22 @@ def tile_picked_candduel_none_po_kernel(
         def make_z(q):
             nc.vector.scalar_tensor_tensor(zb[q][:], hb[q][:].rearrange("p t n -> p n t"), 0.0, gains, ALU.max, ALU.mult)
 
-        def make_z_aside(q):
-            hr = sb(f"hr{q}", [P, NQ, PACK], F32)
-            nc.scalar.activation(hr[:], hb[q][:].rearrange("p t n -> p n t"), ACT.Relu)
-            nc.gpsimd.tensor_tensor(zb[q][:], hr[:], gains, ALU.mult)
-
         def quant_z(q):
             nc.vector.quantize_mx(
                 out=zw[q][:].bitcast(FP8X4), scales=zs[q][:], in_=zb[q][:].rearrange("p n t -> p (n t)")
             )
 
-        make_z_aside(2)
-        make_z_aside(3)
-        make_z(0)
-        nc.vector.tensor_copy(cw_first[:], cw[:, 0:C:PACK])
+        hp = sb("hp", [P, PACK, NQ], F32)
+        zp = sb("zp", [P, PACK, NQ], BF16)
+        nc.scalar.activation(hp[:], hb[0][:], ACT.Relu)
+        for t in range(PACK):
+            nc.scalar.activation(zp[:, t, :], hp[:, t, :], ACT.Copy, scale=gs_t[:, t : t + 1])
+        nc.scalar.copy(zb[0][:], zp[:].rearrange("p t n -> p n t"))
         make_z(1)
-        for q in (0, 2, 1, 3):
+        make_z(2)
+        quant_z(1)
+        make_z(3)
+        for q in (2, 0, 3):
             quant_z(q)
 
         def score(out, words, scales, q):
@@ -140,18 +145,16 @@ def tile_picked_candduel_none_po_kernel(
 
         early = (nq - 1) * NQ
         s_early = psum.tile([P, early], F32, name="s_early")
-        for q in (0, 2, 1):
+        for q in (1, 2, 0):
             score(s_early[:, NQ * q : NQ * (q + 1)], cw_first[:], cs_first[:], q)
-        s_late = psum.tile([P, NQ], F32, name="s_late", tag="bank2")
+        s_late = psum.tile([P, NQ], F32, name="s_late", tag="bank0")
         score(s_late[:], cw_first[:], cs_first[:], nq - 1)
 
         rest = PACK - 1
-        cs_rest = sb("cs_rest", [P, rest * P], U8, tag="zb1")
+        cs_rest = sb("cs_rest", [P, rest * P], U8, tag="zb0")
         cw_rest = sb("cw_rest", [P, rest * P], U32, tag=f"zb{nq - 1}")
-        for dst, src in ((cs_rest, cs), (cw_rest, cw)):
-            nc.vector.tensor_copy(
-                dst[:].rearrange("p (t m) -> p m t", t=rest), src[:].rearrange("p (m t) -> p m t", t=PACK)[:, :, 1:PACK]
-            )
+        deal(cs_rest[:], cs[:], 1)
+        deal(cw_rest[:], cw[:], 1)
         s_bank = {}
         for t in ORDER[1:]:
             s_bank[t] = psum.tile([P, S], F32, name=f"s_bank{t}")
@@ -162,16 +165,8 @@ def tile_picked_candduel_none_po_kernel(
         sw = {t: sb(f"sw{t}", [P, S], F32) for t in ORDER}
         av = {t: sb(f"av{t}", [P, V], F32) for t in ORDER}
         bv = {t: sb(f"bv{t}", [P, V], F32) for t in ORDER}
-        dv = {t: sb(f"dv{t}", [P, V], F32) for t in ORDER}
         ta = {t: sb(f"ta{t}", [P, V], F32) for t in ORDER}
-        tb = {t: sb(f"tb{t}", [P, V], F32) for t in ORDER}
         yw = {t: sb(f"yw{t}", [P, S], F32) for t in ORDER}
-
-        def diff(t):
-            eng = nc.vector if t == ORDER[-1] else nc.gpsimd
-            eng.tensor_tensor(dv[t][:], av[t][:], bv[t][:], ALU.subtract)
-            nc.scalar.activation(ta[t][:], dv[t][:], ACT.Sigmoid)
-            nc.scalar.activation(tb[t][:], dv[t][:], ACT.Sigmoid, scale=-1.0)
 
         for i, t in enumerate(ORDER):
             if i == 0:
@@ -180,12 +175,37 @@ def tile_picked_candduel_none_po_kernel(
             else:
                 nc.scalar.activation(sw[t][:], s_bank[t][:], ACT.Copy, scale=0.0625)
             nc.vector.tensor_copy(av[t][:], sw[t][:].indirect(la_t[:]))
-            if i > 0:
-                diff(ORDER[i - 1])
             nc.vector.tensor_copy(bv[t][:], sw[t][:].indirect(lb_t[:]))
 
+        tb = {}
+        dv = {}
+
+        def weigh_b(t, tag):
+            tb[t] = sb(f"tb{t}", [P, V], F32, tag=tag)
+            nc.scalar.activation(tb[t][:], dv[t][:], ACT.Sigmoid, scale=-1.0)
+
+        for i, t in enumerate(ORDER):
+            turned = psum.tile([P, 2, V], F32, name=f"turned{t}", tag="bank3")
+            for j, src in enumerate((av[t], bv[t])):
+                for u in range(V // P):
+                    nc.tensor.transpose(turned[:, j, P * u : P * (u + 1)], src[:, P * u : P * (u + 1)], ident[:])
+            at = sb(f"at{t}", [P, V], F32)
+            bt = sb(f"bt{t}", [P, V], F32)
+            nc.scalar.activation(at[:], turned[:, 0, :], ACT.Copy)
+            nc.scalar.activation(bt[:], turned[:, 1, :], ACT.Copy, scale=-1.0)
+            dv[t] = psum.tile([P, V], F32, name=f"dv{t}", tag=f"bank{1 + i % 2}")
+            for u in range(V // P):
+                cols = slice(P * u, P * (u + 1))
+                nc.tensor.matmul(dv[t][:, cols], at[:, cols], ident[:], start=True, stop=False, is_transpose=True)
+                nc.tensor.matmul(dv[t][:, cols], bt[:, cols], ident[:], start=False, stop=True, is_transpose=True)
+            nc.scalar.activation(ta[t][:], dv[t][:], ACT.Sigmoid)
+            if i > 0:
+                weigh_b(ORDER[i - 1], f"bt{t}")
+        weigh_b(ORDER[-1], None)
+
         half = S // 2
-        yb = [sb(f"yb{h}", [P, half, PACK], BF16) for h in range(2)]
+        yall = sb("yall", [P, S, PACK], BF16, tag=f"at{ORDER[-1]}")
+        yb = [yall[:, half * h : half * (h + 1), :] for h in range(2)]
         yc = [sb(f"yc{h}", [P, half], I32) for h in range(2)]
         ys = sb("ys", [P, S], U8)
         rows = out_0.rearrange("(p t) c -> p t c", t=PACK)
@@ -206,7 +226,6 @@ def tile_picked_candduel_none_po_kernel(
                     nc.scalar.activation(yb[h][:, :, t], cols, ACT.Copy)
 
         put_a(ORDER[0])
-        diff(ORDER[-1])
         for i in range(1, PACK):
             put_a(ORDER[i])
             put_b(ORDER[i - 1])

@@ -56,11 +56,11 @@ def tile_picked_candduel_none_po_kernel(
         nc.sync.dma_start(offs_t[:], offs)
         nc.sync.dma_start(cand_t[:], cand)
         nc.sync.dma_start(ww[:], w1_words[0].rearrange("p n t -> p (n t)").bitcast(I32))
-        for q in range(QUADS):
-            nc.sync.dma_start(xs[32 * q : 32 * q + 4, :].bitcast(I32), x_scales[0, 4 * q : 4 * q + 4, :].bitcast(I32))
+        for r in range(4):
+            nc.sync.dma_start(xs[r:P:32, :].bitcast(I32), x_scales[0, r:16:4, :].bitcast(I32))
         nc.sync.dma_start(xw[:], x_words[0].rearrange("p n t -> p (n t)").bitcast(I32))
-        for q in range(QUADS):
-            nc.sync.dma_start(ws[32 * q : 32 * q + 4, :].bitcast(I32), w1_scales[0, 4 * q : 4 * q + 4, :].bitcast(I32))
+        for r in range(4):
+            nc.sync.dma_start(ws[r:P:32, :].bitcast(I32), w1_scales[0, r:16:4, :].bitcast(I32))
         nc.sync.dma_start(gs_t[:], gs.rearrange("(p t) o -> p (t o)", t=PACK))
         nc.sync.dma_start(la_t[:], la)
         nc.sync.dma_start(lb_t[:], lb)
@@ -204,6 +204,7 @@ def tile_picked_candduel_none_po_kernel(
         weigh_b(ORDER[-1], None)
 
         half = S // 2
+        split = 384
         yall = sb("yall", [P, S, PACK], BF16, tag=f"at{ORDER[-1]}")
         yb = [yall[:, half * h : half * (h + 1), :] for h in range(2)]
         yc = [sb(f"yc{h}", [P, half], I32) for h in range(2)]
@@ -216,14 +217,16 @@ def tile_picked_candduel_none_po_kernel(
         def put_b(t):
             nc.vector.tensor_tensor(yw[t][:].indirect(lb_t[:]), bv[t][:], tb[t][:], ALU.mult)
             nc.sync.dma_start(rows[:, t, :], yw[t][:])
-            for h in range(2):
-                cols = yw[t][:, half * h : half * (h + 1)]
-                if t == ORDER[-1] and h == 0:
-                    nc.vector.tensor_copy(yb[h][:, :, t], cols)
-                elif t == ORDER[0] and h == 0:
-                    nc.scalar.activation(yb[h][:, :, 0:2], cols.unsqueeze(2).to_broadcast([P, half, 2]), ACT.Copy)
-                else:
-                    nc.scalar.activation(yb[h][:, :, t], cols, ACT.Copy)
+            if t == ORDER[-1]:
+                nc.vector.tensor_copy(yall[:, 0:half, t], yw[t][:, 0:half])
+                nc.vector.tensor_copy(yall[:, half:split, t], yw[t][:, half:split])
+                nc.scalar.activation(yall[:, split:S, t], yw[t][:, split:S], ACT.Copy)
+            elif t == ORDER[0]:
+                both = yw[t][:, 0:split].unsqueeze(2).to_broadcast([P, split, 2])
+                nc.scalar.activation(yall[:, 0:split, 0:2], both, ACT.Copy)
+                nc.scalar.activation(yall[:, split:S, t], yw[t][:, split:S], ACT.Copy)
+            else:
+                nc.scalar.activation(yall[:, :, t], yw[t][:], ACT.Copy)
 
         put_a(ORDER[0])
         for i in range(1, PACK):

from contextlib import ExitStack

import concourse.mybir as mybir
from concourse.masks import make_identity

K, T, S, V, H, C = 512, 2048, 512, 256, 512, 512
FLOPS = 2 * K * H * S + 2 * K * C * S

F32 = mybir.dt.float32
BF16 = mybir.dt.bfloat16
I32 = mybir.dt.int32
U32 = mybir.dt.uint32
U16 = mybir.dt.uint16
U8 = mybir.dt.uint8
FP8X4 = mybir.dt.float8_e4m3fn_x4
ALU = mybir.AluOpType
ACT = mybir.ActivationFunctionType

P = 128
PACK = 4
QUADS = 4
NQ = 128
ORDER = (0, 2, 3, 1)


def tile_picked_candduel_none_po_kernel(
    tc, x_words, x_scales, w1_words, w1_scales, gs, offs, cand, la, lb, out_0, out_1, out_2
):
    nc = tc.nc
    with ExitStack() as ctx:
        keep = ctx.enter_context(tc.tile_pool(name="keep", bufs=1))
        psum = ctx.enter_context(tc.psum_pool(name="psum", bufs=1))

        def sb(name, shape, dtype, tag=None):
            return keep.tile(shape, dtype, name=name, tag=tag or name, align_bytes=64)

        offs_t = sb("offs_t", [P, S // 16], U16)
        cand_t = sb("cand_t", [P, C // 16], U16)
        la_t = sb("la_t", [P, V // 16], U16)
        lb_t = sb("lb_t", [P, V // 16], U16)
        xw = sb("xw", [P, T], I32)
        xs = sb("xs", [P, T], U8)
        ww = sb("ww", [P, H], I32)
        ws = sb("ws", [P, H], U8)
        gs_t = sb("gs_t", [P, PACK], F32)
        warm = sb("warm", [P, 2], F32)

        nc.vector.memset(xs[:].bitcast(I32), 0)
        nc.vector.memset(ws[:].bitcast(I32), 0)
        nc.vector.memset(warm[:, 0:1], 0.0)
        nc.scalar.activation(warm[:, 1:2], warm[:, 0:1], ACT.Sigmoid)

        ident = sb("ident", [P, P], F32, tag="warm")
        make_identity(nc, ident[:])

        nc.sync.dma_start(offs_t[:], offs)
        nc.sync.dma_start(cand_t[:], cand)
        nc.sync.dma_start(ww[:], w1_words[0].rearrange("p n t -> p (n t)").bitcast(I32))
        for r in range(4):
            nc.sync.dma_start(xs[r:P:32, :].bitcast(I32), x_scales[0, r:16:4, :].bitcast(I32))
        nc.sync.dma_start(xw[:], x_words[0].rearrange("p n t -> p (n t)").bitcast(I32))
        for r in range(4):
            nc.sync.dma_start(ws[r:P:32, :].bitcast(I32), w1_scales[0, r:16:4, :].bitcast(I32))
        nc.sync.dma_start(gs_t[:], gs.rearrange("(p t) o -> p (t o)", t=PACK))
        nc.sync.dma_start(la_t[:], la)
        nc.sync.dma_start(lb_t[:], lb)

        def deal(dst, src, first):
            nc.vector.tensor_copy(
                dst.rearrange("p (t m) -> p m t", m=P), src.rearrange("p (m t) -> p m t", t=PACK)[:, :, first:PACK]
            )

        wwd = sb("wwd", [P, H], I32)
        wsd = sb("wsd", [P, H], U8)
        qs = sb("qs", [P, S], U8)
        cs = sb("cs", [P, C], U8)
        cs_first = sb("cs_first", [P, P], U8)
        cw_first = sb("cw_first", [P, P], U32)

        deal(wwd[:], ww[:], 0)
        nc.vector.tensor_copy(qs[:], xs[:].indirect(offs_t[:]))
        nc.vector.tensor_copy(cs[:], xs[:].indirect(cand_t[:]))
        qw = {0: sb("qw0", [P, S // 2], U32)}
        nc.vector.tensor_copy(qw[0][:], xw[:].bitcast(U32).indirect(offs_t[:, 0:16]))
        deal(wsd[:], ws[:], 0)
        later = sb("later", [P, S // 2 + C], U32, tag="ws")
        qw[1] = later[:, 0 : S // 2]
        cw = later[:, S // 2 :]
        nc.vector.tensor_copy(qw[1][:], xw[:].bitcast(U32).indirect(offs_t[:, 16:32]))
        nc.vector.tensor_copy(cw[:], xw[:].bitcast(U32).indirect(cand_t[:]))
        nc.vector.tensor_copy(cs_first[:], cs[:, 0:C:PACK])
        nc.vector.tensor_copy(cw_first[:], cw[:, 0:C:PACK])

        nq = S // NQ
        hb = {}
        for q in range(nq):
            hb[q] = psum.tile([P, PACK, NQ], F32, name=f"hb{q}", tag=f"bank{q}")
            for t in range(PACK):
                nc.tensor.matmul_mx(
                    out=hb[q][:, t, :],
                    lhsT=wwd[:, P * t : P * (t + 1)].bitcast(FP8X4),
                    lhsT_scale=wsd[:, P * t : P * (t + 1)],
                    rhs=qw[q // 2][:, NQ * (q % 2) : NQ * (q % 2 + 1)].bitcast(FP8X4),
                    rhs_scale=qs[:, NQ * q : NQ * (q + 1)],
                    start=True,
                    stop=True,
                )

        zb = [sb(f"zb{q}", [P, NQ, PACK], BF16) for q in range(nq)]
        zw = [sb(f"zw{q}", [P, NQ], U32) for q in range(nq)]
        zs = [sb(f"zs{q}", [P, NQ], U8) for q in range(nq)]
        gains = gs_t[:].unsqueeze(1).to_broadcast([P, NQ, PACK])

        def make_z(q):
            nc.vector.scalar_tensor_tensor(zb[q][:], hb[q][:].rearrange("p t n -> p n t"), 0.0, gains, ALU.max, ALU.mult)

        def quant_z(q):
            nc.vector.quantize_mx(
                out=zw[q][:].bitcast(FP8X4), scales=zs[q][:], in_=zb[q][:].rearrange("p n t -> p (n t)")
            )

        hp = sb("hp", [P, PACK, NQ], F32)
        zp = sb("zp", [P, PACK, NQ], BF16)
        nc.scalar.activation(hp[:], hb[0][:], ACT.Relu)
        for t in range(PACK):
            nc.scalar.activation(zp[:, t, :], hp[:, t, :], ACT.Copy, scale=gs_t[:, t : t + 1])
        nc.scalar.copy(zb[0][:], zp[:].rearrange("p t n -> p n t"))
        make_z(1)
        make_z(2)
        quant_z(1)
        make_z(3)
        for q in (2, 0, 3):
            quant_z(q)

        def score(out, words, scales, q):
            nc.tensor.matmul_mx(
                out=out,
                lhsT=words.bitcast(FP8X4),
                lhsT_scale=scales,
                rhs=zw[q][:].bitcast(FP8X4),
                rhs_scale=zs[q][:],
                start=True,
                stop=True,
            )

        early = (nq - 1) * NQ
        s_early = psum.tile([P, early], F32, name="s_early")
        for q in (1, 2, 0):
            score(s_early[:, NQ * q : NQ * (q + 1)], cw_first[:], cs_first[:], q)
        s_late = psum.tile([P, NQ], F32, name="s_late", tag="bank0")
        score(s_late[:], cw_first[:], cs_first[:], nq - 1)

        rest = PACK - 1
        cs_rest = sb("cs_rest", [P, rest * P], U8, tag="zb0")
        cw_rest = sb("cw_rest", [P, rest * P], U32, tag=f"zb{nq - 1}")
        deal(cs_rest[:], cs[:], 1)
        deal(cw_rest[:], cw[:], 1)
        s_bank = {}
        for t in ORDER[1:]:
            s_bank[t] = psum.tile([P, S], F32, name=f"s_bank{t}")
            cols = slice(P * (t - 1), P * t)
            for q in range(nq):
                score(s_bank[t][:, NQ * q : NQ * (q + 1)], cw_rest[:, cols], cs_rest[:, cols], q)

        sw = {t: sb(f"sw{t}", [P, S], F32) for t in ORDER}
        av = {t: sb(f"av{t}", [P, V], F32) for t in ORDER}
        bv = {t: sb(f"bv{t}", [P, V], F32) for t in ORDER}
        ta = {t: sb(f"ta{t}", [P, V], F32) for t in ORDER}
        yw = {t: sb(f"yw{t}", [P, S], F32) for t in ORDER}

        for i, t in enumerate(ORDER):
            if i == 0:
                nc.scalar.activation(sw[t][:, 0:early], s_early[:], ACT.Copy, scale=0.0625)
                nc.scalar.activation(sw[t][:, early:S], s_late[:], ACT.Copy, scale=0.0625)
            else:
                nc.scalar.activation(sw[t][:], s_bank[t][:], ACT.Copy, scale=0.0625)
            nc.vector.tensor_copy(av[t][:], sw[t][:].indirect(la_t[:]))
            nc.vector.tensor_copy(bv[t][:], sw[t][:].indirect(lb_t[:]))

        tb = {}
        dv = {}

        def weigh_b(t, tag):
            tb[t] = sb(f"tb{t}", [P, V], F32, tag=tag)
            nc.scalar.activation(tb[t][:], dv[t][:], ACT.Sigmoid, scale=-1.0)

        for i, t in enumerate(ORDER):
            turned = psum.tile([P, 2, V], F32, name=f"turned{t}", tag="bank3")
            for j, src in enumerate((av[t], bv[t])):
                for u in range(V // P):
                    nc.tensor.transpose(turned[:, j, P * u : P * (u + 1)], src[:, P * u : P * (u + 1)], ident[:])
            at = sb(f"at{t}", [P, V], F32)
            bt = sb(f"bt{t}", [P, V], F32)
            nc.scalar.activation(at[:], turned[:, 0, :], ACT.Copy)
            nc.scalar.activation(bt[:], turned[:, 1, :], ACT.Copy, scale=-1.0)
            dv[t] = psum.tile([P, V], F32, name=f"dv{t}", tag=f"bank{1 + i % 2}")
            for u in range(V // P):
                cols = slice(P * u, P * (u + 1))
                nc.tensor.matmul(dv[t][:, cols], at[:, cols], ident[:], start=True, stop=False, is_transpose=True)
                nc.tensor.matmul(dv[t][:, cols], bt[:, cols], ident[:], start=False, stop=True, is_transpose=True)
            nc.scalar.activation(ta[t][:], dv[t][:], ACT.Sigmoid)
            if i > 0:
                weigh_b(ORDER[i - 1], f"bt{t}")
        weigh_b(ORDER[-1], None)

        half = S // 2
        split = 384
        yall = sb("yall", [P, S, PACK], BF16, tag=f"at{ORDER[-1]}")
        yb = [yall[:, half * h : half * (h + 1), :] for h in range(2)]
        yc = [sb(f"yc{h}", [P, half], I32) for h in range(2)]
        ys = sb("ys", [P, S], U8)
        rows = out_0.rearrange("(p t) c -> p t c", t=PACK)

        def put_a(t):
            nc.vector.tensor_tensor(yw[t][:].indirect(la_t[:]), av[t][:], ta[t][:], ALU.mult)

        def put_b(t):
            nc.vector.tensor_tensor(yw[t][:].indirect(lb_t[:]), bv[t][:], tb[t][:], ALU.mult)
            nc.sync.dma_start(rows[:, t, :], yw[t][:])
            if t == ORDER[-1]:
                nc.vector.tensor_copy(yall[:, 0:half, t], yw[t][:, 0:half])
                nc.vector.tensor_copy(yall[:, half:split, t], yw[t][:, half:split])
                nc.scalar.activation(yall[:, split:S, t], yw[t][:, split:S], ACT.Copy)
            elif t == ORDER[0]:
                both = yw[t][:, 0:split].unsqueeze(2).to_broadcast([P, split, 2])
                nc.scalar.activation(yall[:, 0:split, 0:2], both, ACT.Copy)
                nc.scalar.activation(yall[:, split:S, t], yw[t][:, split:S], ACT.Copy)
            else:
                nc.scalar.activation(yall[:, :, t], yw[t][:], ACT.Copy)

        put_a(ORDER[0])
        for i in range(1, PACK):
            put_a(ORDER[i])
            put_b(ORDER[i - 1])
        put_b(ORDER[-1])

        words_out = out_1[0].rearrange("p m t -> p (m t)").bitcast(I32)
        for h in range(2):
            nc.vector.quantize_mx(
                out=yc[h][:].bitcast(FP8X4),
                scales=ys[:, half * h : half * (h + 1)],
                in_=yb[h][:].rearrange("p n t -> p (n t)"),
            )
            nc.sync.dma_start(words_out[:, half * h : half * (h + 1)], yc[h][:])
        for q in range(QUADS):
            eng = nc.scalar if q % 2 else nc.sync
            eng.dma_start(out_2[0, 4 * q : 4 * q + 4, :].bitcast(I32), ys[32 * q : 32 * q + 4, :].bitcast(I32))
